import numpy as np
import ml_dtypes


def mxq(x, axis, fmt="e4m3"):
    dtype, down = {"e4m3": (ml_dtypes.float8_e4m3fn, 7), "e5m2": (ml_dtypes.float8_e5m2, 14)}[fmt]
    v = np.moveaxis(np.asarray(x, np.float32).astype(ml_dtypes.bfloat16).astype(np.float64), axis, -1)
    blocks = v.reshape(v.shape[:-1] + (-1, 32))
    amax = np.abs(blocks).max(-1, keepdims=True)
    byte = np.maximum(np.where(amax > 0, np.frexp(amax)[1] - 1 + 127, 0) - down, 1)
    scale = np.exp2(byte - 127.0)
    codes = (blocks / scale).astype(np.float32).astype(dtype).astype(np.float64)
    return np.moveaxis((codes * scale).reshape(v.shape), -1, axis)


WIDE = False


def mx_kscale(k):
    if not WIDE:
        return np.ones(k)
    levels = np.array([10, -10, 5, -5, 0])
    if k % 512:
        return np.exp2(np.random.permutation(np.resize(levels, k // 32))).repeat(32)
    a = np.empty((k // 512, 16))
    for p in range(k // 512):
        a[p, :8] = np.random.permutation(np.resize(levels, 8))
        for g in range(8):
            far = levels[np.abs(levels - a[p, g]) >= 10]
            a[p, g + 8] = far[np.random.randint(len(far))]
    return np.exp2(a.ravel()).repeat(32)


def f64(x):
    return np.asarray(x).astype(np.float64)


def striped(idx):
    return np.tile(idx.reshape(-1, 16).T, (8, 1)).astype(np.uint16)


def unstriped(offs):
    return offs[:16].T.reshape(-1).astype(np.int64)


def pack_weight(w):
    k, n = w.shape
    w = f64(np.asarray(w, np.float32).astype(ml_dtypes.bfloat16)).reshape(k // 32, 32, n)
    amax = np.abs(w).max(1)
    byte = np.clip(np.where(amax > 0, np.frexp(amax)[1] - 1 + 127 - 7, 1), 1, 254)
    scaled = (w * np.exp2(127.0 - byte)[:, None, :]).reshape(k, n).astype(np.float32)
    words = np.ascontiguousarray(scaled.reshape(k // 512, 128, 4, n).transpose(0, 1, 3, 2)).astype(ml_dtypes.float8_e4m3fn).view(np.uint8)
    return words, np.ascontiguousarray(byte.astype(np.uint8).reshape(k // 512, 16, n))


def unpack_weight(words, scales):
    g, p, n, _ = words.shape
    vals = np.ascontiguousarray(words).view(ml_dtypes.float8_e4m3fn).astype(np.float64) * np.repeat(np.exp2(scales.astype(np.float64) - 127.0), 8, axis=1)[..., None]
    return vals.transpose(0, 1, 3, 2).reshape(g * 512, n)


def sigmoid(v):
    return 1.0 / (1.0 + np.exp(-np.maximum(v, -700.0)))


K, T, S, D, N, H, V, U = 512, 2048, 512, 2, 128, 512, 256, 512


def setup_inputs():
    n = np.random.standard_normal
    s = mx_kscale(K)[:, None]
    u = mx_kscale(H)
    packed_xT = pack_weight(n((K, T)) * s)
    return {
        "x_words": packed_xT[0],
        "x_scales": packed_xT[1],
        "w1": (n((K, H)) / np.sqrt(K) / s).astype(np.float32),
        "w2": (n((K, H)) / np.sqrt(K) / s).astype(np.float32),
        "unit": (np.random.uniform(0.6, 1.4, (H, 1)) * u[:, None]).astype(np.float32),
        "w3": (n((H, N)) / np.sqrt(H) / u[:, None]).astype(np.float32),
        "offs": striped(np.random.permutation(T)[:S]),
        "root": striped(np.random.permutation(np.concatenate([np.arange(V), np.random.randint(0, V, U - V)]))),
        "leaf": striped(np.random.permutation(np.concatenate([np.arange(V), np.random.randint(0, V, U - V)]))),
        "sib": striped(np.random.permutation(U)),
    }


def reference(x_words, x_scales, w1, w2, unit, w3, offs, root, leaf, sib):
    xq = unpack_weight(x_words, x_scales)[:, unstriped(offs)]
    y = mxq(f64(w1), 0, "e4m3").T @ xq
    ys = mxq(f64(w2), 0, "e4m3").T @ xq
    yg2 = y * sigmoid(ys)
    pref = yg2.reshape(len(yg2), -1, D).sum(axis=2)
    rt_ = pref[:, unstriped(root)]
    lf = pref[:, unstriped(leaf)]
    path = rt_ + lf * np.tanh(rt_)
    hid = f64(unit) * (path - (0.5 * path[:, unstriped(sib)]))
    return mxq(f64(w3), 0, "e4m3").T @ mxq(hid, 0, "e4m3")

@@ -1,0 +1,166 @@
+from contextlib import ExitStack
+
+import concourse.mybir as mybir
+
+K, T, S, H, V, U, N = 512, 2048, 512, 512, 256, 512, 128
+FLOPS = 2 * (2 * K * H * S + H * N * U)
+
+F32 = mybir.dt.float32
+BF16 = mybir.dt.bfloat16
+I32 = mybir.dt.int32
+U32 = mybir.dt.uint32
+U16 = mybir.dt.uint16
+U8 = mybir.dt.uint8
+FP8X4 = mybir.dt.float8_e4m3fn_x4
+ACT = mybir.ActivationFunctionType
+ALU = mybir.AluOpType
+
+P = 128
+PACK = 4
+W2_CHUNKS = ((0, 256), (256, 512))
+W1_CHUNKS = ((0, 256), (256, 512))
+PIECES = ((0, 256), (256, 512))
+
+
+def tile_picked_yprefsh_sib_p_kernel(
+    tc, x_words, x_scales, w1, w2, unit, w3, offs, root, leaf, sib, out
+):
+    nc = tc.nc
+    with ExitStack() as ctx:
+        sb = ctx.enter_context(tc.tile_pool(name="sb", bufs=1))
+        ps = ctx.enter_context(tc.psum_pool(name="ps", bufs=4))
+
+        def load_list(src, name):
+            tile = sb.tile([P, src.shape[1]], U16, name=name)
+            nc.sync.dma_start(tile[:], src)
+            return tile
+
+        def load_rows(queue, w, cols, parts, name):
+            rows = w.rearrange("(p j) c -> p j c", j=PACK)
+            raw = sb.tile([P, PACK, cols[1] - cols[0]], F32, name=name)
+            step = PACK // parts
+            for j in range(0, PACK, step):
+                queue.dma_start(raw[:, j : j + step, :], rows[:, j : j + step, cols[0] : cols[1]])
+            return raw
+
+        offs_sb = load_list(offs, "offs_sb")
+        w2_raw = [
+            load_rows(nc.scalar, w2, W2_CHUNKS[0], 2, "w2_raw0"),
+            load_rows(nc.scalar, w2, W2_CHUNKS[1], 1, "w2_raw1"),
+        ]
+        root_sb = load_list(root, "root_sb")
+        leaf_sb = load_list(leaf, "leaf_sb")
+        sib_sb = load_list(sib, "sib_sb")
+        unit_sb = sb.tile([P, PACK], F32, name="unit_sb")
+        nc.sync.dma_start(unit_sb[:], unit.rearrange("(p t) o -> p (t o)", t=PACK))
+        scales = sb.tile([P, T], U8, name="scales")
+        nc.vector.memset(scales[:].bitcast(I32), 0)
+        for q in range(4):
+            nc.sync.dma_start(
+                scales[32 * q : 32 * q + 4, :].bitcast(I32), x_scales[0, 4 * q : 4 * q + 4, :].bitcast(I32)
+            )
+        words = sb.tile([P, T], U32, name="words")
+        nc.sync.dma_start(words[:].bitcast(I32), x_words[0].rearrange("p c r -> p (c r)").bitcast(I32))
+        w1_raw = [load_rows(nc.sync, w1, cols, 1, "w1_raw%d" % cols[0]) for cols in W1_CHUNKS]
+        w3_raw = load_rows(nc.sync, w3, (0, N), 1, "w3_raw")
+
+        def round_and_deal(raws, chunks, name):
+            dealt = sb.tile([P, PACK * H], BF16, name=name, align_bytes=64)
+            view = dealt[:].rearrange("p (t m j) -> p m j t", t=PACK, j=PACK)
+            for raw, (a, b) in zip(raws, chunks):
+                nc.vector.tensor_copy(
+                    view[:, a // PACK : b // PACK], raw[:].rearrange("p j (m t) -> p m j t", t=PACK)
+                )
+            return dealt
+
+        def quantize(values, width, name):
+            codes = sb.tile([P, width], U32, name=name + "_codes", align_bytes=64)
+            scale = sb.tile([P, width], U8, name=name + "_scale", align_bytes=64)
+            nc.vector.quantize_mx(codes[:].bitcast(FP8X4), scale[:], values)
+            return codes[:].bitcast(FP8X4), scale[:]
+
+        def product(lhs, rhs, width, tag):
+            acc = ps.tile([P, width], F32, name=tag)
+            nc.tensor.matmul_mx(
+                acc[:], lhsT=lhs[0], lhsT_scale=lhs[1], rhs=rhs[0], rhs_scale=rhs[1], start=True, stop=True
+            )
+            return acc
+
+        x_codes = sb.tile([P, S], U32, name="x_codes", align_bytes=64)
+        x_bytes = sb.tile([P, S], U8, name="x_bytes", align_bytes=64)
+        x_mx = (x_codes[:].bitcast(FP8X4), x_bytes[:])
+        w2_dealt = round_and_deal(w2_raw, W2_CHUNKS, "w2_dealt")
+        w2_codes, w2_scale = quantize(w2_dealt[:], H, "w2")
+        nc.vector.tensor_copy(x_bytes[:], scales[:].indirect(offs_sb[:]))
+        nc.vector.tensor_copy(x_codes[:], words[:].indirect(offs_sb[:]))
+
+        leaf_win = []
+        for t in range(PACK):
+            cols = slice(t * P, (t + 1) * P)
+            ys = product((w2_codes[:, cols], w2_scale[:, cols]), x_mx, S, "ys")
+            win = sb.tile([P, V + S], F32, name="leaf_win%d" % t)
+            nc.scalar.activation(win[:, V:], ys[:], ACT.Sigmoid)
+            leaf_win.append(win)
+
+        w1_dealt = round_and_deal(w1_raw, W1_CHUNKS, "w1_dealt")
+        y = []
+        for t in range(PACK):
+            w1_mx = quantize(w1_dealt[:, t * PACK * P : (t + 1) * PACK * P], P, "w1_%d" % t)
+            y.append(product(w1_mx, x_mx, S, "y"))
+
+        path = sb.tile([P, PACK, U], F32, name="path")
+        pulled = [sb.tile([P, PACK, b - a], F32, name="pulled%d" % a) for a, b in PIECES]
+        rt = [sb.tile([P, U], F32, name="rt%d" % t) for t in range(PACK)]
+        bound = [sb.tile([P, U], F32, name="bound%d" % t) for t in range(PACK)]
+
+        def nodes(t):
+            root_win = sb.tile([P, V + S], F32, name="root_win%d" % t)
+            nc.vector.tensor_tensor(root_win[:, V:], y[t][:], leaf_win[t][:, V:], ALU.mult)
+            nc.vector.tensor_tensor(root_win[:, :V], root_win[:, V::2], root_win[:, V + 1 :: 2], ALU.add)
+            nc.vector.tensor_scalar(leaf_win[t][:, :V], root_win[:, :V], unit_sb[:, t : t + 1], None, ALU.mult)
+            nc.scalar.activation(rt[t][:], root_win[:].indirect(root_sb[:]), ACT.Copy)
+            nc.scalar.activation(bound[t][:], rt[t][:], ACT.Tanh)
+
+        def paths(t):
+            weighted = sb.tile([P, U], F32, name="weighted%d" % t)
+            nc.vector.tensor_tensor(weighted[:], leaf_win[t][:].indirect(leaf_sb[:]), bound[t][:], ALU.mult)
+            nc.vector.scalar_tensor_tensor(
+                path[:, t, :], rt[t][:], unit_sb[:, t : t + 1], weighted[:], ALU.mult, ALU.add
+            )
+
+        def siblings(t):
+            for piece, (a, b) in zip(pulled, PIECES):
+                nc.scalar.activation(
+                    piece[:, t, :], path[:, t, :].indirect(sib_sb[:, a // 16 : b // 16]), ACT.Copy, scale=-0.5
+                )
+
+        nodes(0)
+        nodes(1)
+        nodes(2)
+        paths(0)
+        nodes(3)
+        for t in range(1, PACK):
+            paths(t)
+        for t in range(PACK):
+            siblings(t)
+
+        w3_bf = sb.tile([P, N * PACK], BF16, name="w3_bf", align_bytes=64)
+        nc.vector.tensor_copy(
+            w3_bf[:].rearrange("p (c i j) -> p c j i", i=4, j=PACK),
+            w3_raw[:].rearrange("p j (c i) -> p c j i", i=4),
+        )
+        w3_mx = quantize(w3_bf[:], N, "w3")
+
+        for piece, (a, b) in zip(pulled, PIECES):
+            n = b - a
+            hid = sb.tile([P, n * PACK], BF16, name="hid%d" % a, align_bytes=64)
+            nc.vector.tensor_tensor(
+                hid[:].rearrange("p (c i t) -> p c t i", i=4, t=PACK),
+                path[:, :, a:b].rearrange("p t (c i) -> p c t i", i=4),
+                piece[:].rearrange("p t (c i) -> p c t i", i=4),
+                ALU.add,
+            )
+            acc = product(w3_mx, quantize(hid[:], n, "hid%d" % a), n, "ys")
+            res = sb.tile([P, n], F32, name="res%d" % a)
+            nc.scalar.copy(res[:], acc[:])
+            nc.sync.dma_start(out[:, a:b], res[:])

@@ -16,10 +16,11 @@ ACT = mybir.ActivationFunctionType
 ALU = mybir.AluOpType
 
 P = 128
+GATED_AT = (S // 2, 0, S, 2 * S)
+SMALLEST_NORMAL = 2.0**-126
 PACK = 4
-W2_CHUNKS = ((0, 256), (256, 512))
-W1_CHUNKS = ((0, 256), (256, 512))
-PIECES = ((0, 256), (256, 512))
+CHUNKS = ((0, 256), (256, 512))
+PIECES = ((0, 128), (128, 384), (384, 512))
 
 
 def tile_picked_yprefsh_sib_p_kernel(
@@ -35,34 +36,29 @@ def tile_picked_yprefsh_sib_p_kernel(
             nc.sync.dma_start(tile[:], src)
             return tile
 
-        def load_rows(queue, w, cols, parts, name):
+        def load_rows(w, cols, name):
             rows = w.rearrange("(p j) c -> p j c", j=PACK)
             raw = sb.tile([P, PACK, cols[1] - cols[0]], F32, name=name)
-            step = PACK // parts
-            for j in range(0, PACK, step):
-                queue.dma_start(raw[:, j : j + step, :], rows[:, j : j + step, cols[0] : cols[1]])
+            nc.sync.dma_start(raw[:], rows[:, :, cols[0] : cols[1]])
             return raw
 
+        scales = sb.tile([P, T], U8, name="scales", tag="scales_then_codes", align_bytes=64)
+        nc.vector.memset(scales[:].bitcast(I32), 0)
+        for q in range(4):
+            nc.scalar.dma_start(
+                scales[32 * q : 32 * q + 4, :].bitcast(I32), x_scales[0, 4 * q : 4 * q + 4, :].bitcast(I32)
+            )
         offs_sb = load_list(offs, "offs_sb")
-        w2_raw = [
-            load_rows(nc.scalar, w2, W2_CHUNKS[0], 2, "w2_raw0"),
-            load_rows(nc.scalar, w2, W2_CHUNKS[1], 1, "w2_raw1"),
-        ]
+        w2_raw = [load_rows(w2, cols, "w2_raw%d" % cols[0]) for cols in CHUNKS]
+        unit_sb = sb.tile([P, PACK], F32, name="unit_sb")
+        nc.sync.dma_start(unit_sb[:], unit.rearrange("(p t) o -> p (t o)", t=PACK))
+        words = sb.tile([P, T], U32, name="words")
+        nc.sync.dma_start(words[:].bitcast(I32), x_words[0].rearrange("p c r -> p (c r)").bitcast(I32))
+        w1_raw = [load_rows(w1, cols, "w1_raw%d" % cols[0]) for cols in CHUNKS]
         root_sb = load_list(root, "root_sb")
         leaf_sb = load_list(leaf, "leaf_sb")
         sib_sb = load_list(sib, "sib_sb")
-        unit_sb = sb.tile([P, PACK], F32, name="unit_sb")
-        nc.sync.dma_start(unit_sb[:], unit.rearrange("(p t) o -> p (t o)", t=PACK))
-        scales = sb.tile([P, T], U8, name="scales")
-        nc.vector.memset(scales[:].bitcast(I32), 0)
-        for q in range(4):
-            nc.sync.dma_start(
-                scales[32 * q : 32 * q + 4, :].bitcast(I32), x_scales[0, 4 * q : 4 * q + 4, :].bitcast(I32)
-            )
-        words = sb.tile([P, T], U32, name="words")
-        nc.sync.dma_start(words[:].bitcast(I32), x_words[0].rearrange("p c r -> p (c r)").bitcast(I32))
-        w1_raw = [load_rows(nc.sync, w1, cols, 1, "w1_raw%d" % cols[0]) for cols in W1_CHUNKS]
-        w3_raw = load_rows(nc.sync, w3, (0, N), 1, "w3_raw")
+        w3_raw = load_rows(w3, (0, N), "w3_raw")
 
         def round_and_deal(raws, chunks, name):
             dealt = sb.tile([P, PACK * H], BF16, name=name, align_bytes=64)
@@ -86,63 +82,69 @@ def tile_picked_yprefsh_sib_p_kernel(
             )
             return acc
 
-        x_codes = sb.tile([P, S], U32, name="x_codes", align_bytes=64)
+        x_codes = sb.tile([P, S], U32, name="x_codes", tag="scales_then_codes", align_bytes=64)
         x_bytes = sb.tile([P, S], U8, name="x_bytes", align_bytes=64)
         x_mx = (x_codes[:].bitcast(FP8X4), x_bytes[:])
-        w2_dealt = round_and_deal(w2_raw, W2_CHUNKS, "w2_dealt")
+        w2_dealt = round_and_deal(w2_raw, CHUNKS, "w2_dealt")
         w2_codes, w2_scale = quantize(w2_dealt[:], H, "w2")
         nc.vector.tensor_copy(x_bytes[:], scales[:].indirect(offs_sb[:]))
         nc.vector.tensor_copy(x_codes[:], words[:].indirect(offs_sb[:]))
 
-        leaf_win = []
-        for t in range(PACK):
-            cols = slice(t * P, (t + 1) * P)
-            ys = product((w2_codes[:, cols], w2_scale[:, cols]), x_mx, S, "ys")
-            win = sb.tile([P, V + S], F32, name="leaf_win%d" % t)
-            nc.scalar.activation(win[:, V:], ys[:], ACT.Sigmoid)
-            leaf_win.append(win)
+        size = sb.tile([P, PACK], F32, name="size")
+        nc.vector.scalar_tensor_tensor(size[:], unit_sb[:], -1.0, unit_sb[:], ALU.mult, ALU.max)
+        divisor = sb.tile([P, PACK], F32, name="divisor")
+        nc.vector.scalar_tensor_tensor(divisor[:], size[:], SMALLEST_NORMAL, unit_sb[:], ALU.is_lt, ALU.add)
+        per_unit = sb.tile([P, PACK], F32, name="per_unit")
+        nc.vector.reciprocal(per_unit[:], divisor[:])
 
-        w1_dealt = round_and_deal(w1_raw, W1_CHUNKS, "w1_dealt")
-        y = []
-        for t in range(PACK):
-            w1_mx = quantize(w1_dealt[:, t * PACK * P : (t + 1) * PACK * P], P, "w1_%d" % t)
-            y.append(product(w1_mx, x_mx, S, "y"))
+        w1_dealt = round_and_deal(w1_raw, CHUNKS, "w1_dealt")
+        w1_mx = [
+            quantize(w1_dealt[:, t * PACK * P : (t + 1) * PACK * P], P, "w1_%d" % t) for t in range(PACK)
+        ]
 
         path = sb.tile([P, PACK, U], F32, name="path")
         pulled = [sb.tile([P, PACK, b - a], F32, name="pulled%d" % a) for a, b in PIECES]
         rt = [sb.tile([P, U], F32, name="rt%d" % t) for t in range(PACK)]
         bound = [sb.tile([P, U], F32, name="bound%d" % t) for t in range(PACK)]
 
+        window = [sb.tile([P, V + S], F32, name="window%d" % t) for t in range(PACK)]
+
+        gated = sb.tile([P, 3 * S], F32, name="gated")
+
         def nodes(t):
-            root_win = sb.tile([P, V + S], F32, name="root_win%d" % t)
-            nc.vector.tensor_tensor(root_win[:, V:], y[t][:], leaf_win[t][:, V:], ALU.mult)
-            nc.vector.tensor_tensor(root_win[:, :V], root_win[:, V::2], root_win[:, V + 1 :: 2], ALU.add)
-            nc.vector.tensor_scalar(leaf_win[t][:, :V], root_win[:, :V], unit_sb[:, t : t + 1], None, ALU.mult)
-            nc.scalar.activation(rt[t][:], root_win[:].indirect(root_sb[:]), ACT.Copy)
-            nc.scalar.activation(bound[t][:], rt[t][:], ACT.Tanh)
+            cols = slice(t * P, (t + 1) * P)
+            ys = product((w2_codes[:, cols], w2_scale[:, cols]), x_mx, S, "ys")
+            win = window[t]
+            nc.scalar.activation(win[:, V:], ys[:], ACT.Sigmoid)
+            y = product(w1_mx[t], x_mx, S, "y")
+            at = GATED_AT[t]
+            nc.vector.scalar_tensor_tensor(
+                gated[:, at : at + S], y[:], unit_sb[:, t : t + 1], win[:, V:], ALU.mult, ALU.mult
+            )
+            nc.vector.tensor_tensor(
+                win[:, :V], gated[:, at : at + S : 2], gated[:, at + 1 : at + S : 2], ALU.add
+            )
+            nc.scalar.activation(rt[t][:], win[:].indirect(root_sb[:]), ACT.Copy)
+            nc.scalar.activation(bound[t][:], rt[t][:], ACT.Tanh, scale=per_unit[:, t : t + 1])
 
         def paths(t):
             weighted = sb.tile([P, U], F32, name="weighted%d" % t)
-            nc.vector.tensor_tensor(weighted[:], leaf_win[t][:].indirect(leaf_sb[:]), bound[t][:], ALU.mult)
-            nc.vector.scalar_tensor_tensor(
-                path[:, t, :], rt[t][:], unit_sb[:, t : t + 1], weighted[:], ALU.mult, ALU.add
+            nc.vector.tensor_tensor(weighted[:], window[t][:].indirect(leaf_sb[:]), bound[t][:], ALU.mult)
+            nc.vector.tensor_tensor(path[:, t, :], rt[t][:], weighted[:], ALU.add)
+
+        def siblings(t, k):
+            a, b = PIECES[k]
+            nc.scalar.activation(
+                pulled[k][:, t, :], path[:, t, :].indirect(sib_sb[:, a // 16 : b // 16]), ACT.Copy, scale=-0.5
             )
 
-        def siblings(t):
-            for piece, (a, b) in zip(pulled, PIECES):
-                nc.scalar.activation(
-                    piece[:, t, :], path[:, t, :].indirect(sib_sb[:, a // 16 : b // 16]), ACT.Copy, scale=-0.5
-                )
-
-        nodes(0)
-        nodes(1)
-        nodes(2)
-        paths(0)
-        nodes(3)
-        for t in range(1, PACK):
-            paths(t)
         for t in range(PACK):
-            siblings(t)
+            nodes(t)
+        for t in range(PACK):
+            paths(t)
+        for k in range(len(PIECES)):
+            for t in range(PACK):
+                siblings(t, k)
 
         w3_bf = sb.tile([P, N * PACK], BF16, name="w3_bf", align_bytes=64)
         nc.vector.tensor_copy(

from contextlib import ExitStack

import concourse.mybir as mybir

K, T, S, H, V, U, N = 512, 2048, 512, 512, 256, 512, 128
FLOPS = 2 * (2 * K * H * S + H * N * U)

F32 = mybir.dt.float32
BF16 = mybir.dt.bfloat16
I32 = mybir.dt.int32
U32 = mybir.dt.uint32
U16 = mybir.dt.uint16
U8 = mybir.dt.uint8
FP8X4 = mybir.dt.float8_e4m3fn_x4
ACT = mybir.ActivationFunctionType
ALU = mybir.AluOpType

P = 128
GATED_AT = (S // 2, 0, S, 2 * S)
SMALLEST_NORMAL = 2.0**-126
PACK = 4
CHUNKS = ((0, 256), (256, 512))
PIECES = ((0, 128), (128, 384), (384, 512))


def tile_picked_yprefsh_sib_p_kernel(
    tc, x_words, x_scales, w1, w2, unit, w3, offs, root, leaf, sib, out
):
    nc = tc.nc
    with ExitStack() as ctx:
        sb = ctx.enter_context(tc.tile_pool(name="sb", bufs=1))
        ps = ctx.enter_context(tc.psum_pool(name="ps", bufs=4))

        def load_list(src, name):
            tile = sb.tile([P, src.shape[1]], U16, name=name)
            nc.sync.dma_start(tile[:], src)
            return tile

        def load_rows(w, cols, name):
            rows = w.rearrange("(p j) c -> p j c", j=PACK)
            raw = sb.tile([P, PACK, cols[1] - cols[0]], F32, name=name)
            nc.sync.dma_start(raw[:], rows[:, :, cols[0] : cols[1]])
            return raw

        scales = sb.tile([P, T], U8, name="scales", tag="scales_then_codes", align_bytes=64)
        nc.vector.memset(scales[:].bitcast(I32), 0)
        for q in range(4):
            nc.scalar.dma_start(
                scales[32 * q : 32 * q + 4, :].bitcast(I32), x_scales[0, 4 * q : 4 * q + 4, :].bitcast(I32)
            )
        offs_sb = load_list(offs, "offs_sb")
        w2_raw = [load_rows(w2, cols, "w2_raw%d" % cols[0]) for cols in CHUNKS]
        unit_sb = sb.tile([P, PACK], F32, name="unit_sb")
        nc.sync.dma_start(unit_sb[:], unit.rearrange("(p t) o -> p (t o)", t=PACK))
        words = sb.tile([P, T], U32, name="words")
        nc.sync.dma_start(words[:].bitcast(I32), x_words[0].rearrange("p c r -> p (c r)").bitcast(I32))
        w1_raw = [load_rows(w1, cols, "w1_raw%d" % cols[0]) for cols in CHUNKS]
        root_sb = load_list(root, "root_sb")
        leaf_sb = load_list(leaf, "leaf_sb")
        sib_sb = load_list(sib, "sib_sb")
        w3_raw = load_rows(w3, (0, N), "w3_raw")

        def round_and_deal(raws, chunks, name):
            dealt = sb.tile([P, PACK * H], BF16, name=name, align_bytes=64)
            view = dealt[:].rearrange("p (t m j) -> p m j t", t=PACK, j=PACK)
            for raw, (a, b) in zip(raws, chunks):
                nc.vector.tensor_copy(
                    view[:, a // PACK : b // PACK], raw[:].rearrange("p j (m t) -> p m j t", t=PACK)
                )
            return dealt

        def quantize(values, width, name):
            codes = sb.tile([P, width], U32, name=name + "_codes", align_bytes=64)
            scale = sb.tile([P, width], U8, name=name + "_scale", align_bytes=64)
            nc.vector.quantize_mx(codes[:].bitcast(FP8X4), scale[:], values)
            return codes[:].bitcast(FP8X4), scale[:]

        def product(lhs, rhs, width, tag):
            acc = ps.tile([P, width], F32, name=tag)
            nc.tensor.matmul_mx(
                acc[:], lhsT=lhs[0], lhsT_scale=lhs[1], rhs=rhs[0], rhs_scale=rhs[1], start=True, stop=True
            )
            return acc

        x_codes = sb.tile([P, S], U32, name="x_codes", tag="scales_then_codes", align_bytes=64)
        x_bytes = sb.tile([P, S], U8, name="x_bytes", align_bytes=64)
        x_mx = (x_codes[:].bitcast(FP8X4), x_bytes[:])
        w2_dealt = round_and_deal(w2_raw, CHUNKS, "w2_dealt")
        w2_codes, w2_scale = quantize(w2_dealt[:], H, "w2")
        nc.vector.tensor_copy(x_bytes[:], scales[:].indirect(offs_sb[:]))
        nc.vector.tensor_copy(x_codes[:], words[:].indirect(offs_sb[:]))

        size = sb.tile([P, PACK], F32, name="size")
        nc.vector.scalar_tensor_tensor(size[:], unit_sb[:], -1.0, unit_sb[:], ALU.mult, ALU.max)
        divisor = sb.tile([P, PACK], F32, name="divisor")
        nc.vector.scalar_tensor_tensor(divisor[:], size[:], SMALLEST_NORMAL, unit_sb[:], ALU.is_lt, ALU.add)
        per_unit = sb.tile([P, PACK], F32, name="per_unit")
        nc.vector.reciprocal(per_unit[:], divisor[:])

        w1_dealt = round_and_deal(w1_raw, CHUNKS, "w1_dealt")
        w1_mx = [
            quantize(w1_dealt[:, t * PACK * P : (t + 1) * PACK * P], P, "w1_%d" % t) for t in range(PACK)
        ]

        path = sb.tile([P, PACK, U], F32, name="path")
        pulled = [sb.tile([P, PACK, b - a], F32, name="pulled%d" % a) for a, b in PIECES]
        rt = [sb.tile([P, U], F32, name="rt%d" % t) for t in range(PACK)]
        bound = [sb.tile([P, U], F32, name="bound%d" % t) for t in range(PACK)]

        window = [sb.tile([P, V + S], F32, name="window%d" % t) for t in range(PACK)]

        gated = sb.tile([P, 3 * S], F32, name="gated")

        def nodes(t):
            cols = slice(t * P, (t + 1) * P)
            ys = product((w2_codes[:, cols], w2_scale[:, cols]), x_mx, S, "ys")
            win = window[t]
            nc.scalar.activation(win[:, V:], ys[:], ACT.Sigmoid)
            y = product(w1_mx[t], x_mx, S, "y")
            at = GATED_AT[t]
            nc.vector.scalar_tensor_tensor(
                gated[:, at : at + S], y[:], unit_sb[:, t : t + 1], win[:, V:], ALU.mult, ALU.mult
            )
            nc.vector.tensor_tensor(
                win[:, :V], gated[:, at : at + S : 2], gated[:, at + 1 : at + S : 2], ALU.add
            )
            nc.scalar.activation(rt[t][:], win[:].indirect(root_sb[:]), ACT.Copy)
            nc.scalar.activation(bound[t][:], rt[t][:], ACT.Tanh, scale=per_unit[:, t : t + 1])

        def paths(t):
            weighted = sb.tile([P, U], F32, name="weighted%d" % t)
            nc.vector.tensor_tensor(weighted[:], window[t][:].indirect(leaf_sb[:]), bound[t][:], ALU.mult)
            nc.vector.tensor_tensor(path[:, t, :], rt[t][:], weighted[:], ALU.add)

        def siblings(t, k):
            a, b = PIECES[k]
            nc.scalar.activation(
                pulled[k][:, t, :], path[:, t, :].indirect(sib_sb[:, a // 16 : b // 16]), ACT.Copy, scale=-0.5
            )

        for t in range(PACK):
            nodes(t)
        for t in range(PACK):
            paths(t)
        for k in range(len(PIECES)):
            for t in range(PACK):
                siblings(t, k)

        w3_bf = sb.tile([P, N * PACK], BF16, name="w3_bf", align_bytes=64)
        nc.vector.tensor_copy(
            w3_bf[:].rearrange("p (c i j) -> p c j i", i=4, j=PACK),
            w3_raw[:].rearrange("p j (c i) -> p c j i", i=4),
        )
        w3_mx = quantize(w3_bf[:], N, "w3")

        for piece, (a, b) in zip(pulled, PIECES):
            n = b - a
            hid = sb.tile([P, n * PACK], BF16, name="hid%d" % a, align_bytes=64)
            nc.vector.tensor_tensor(
                hid[:].rearrange("p (c i t) -> p c t i", i=4, t=PACK),
                path[:, :, a:b].rearrange("p t (c i) -> p c t i", i=4),
                piece[:].rearrange("p t (c i) -> p c t i", i=4),
                ALU.add,
            )
            acc = product(w3_mx, quantize(hid[:], n, "hid%d" % a), n, "ys")
            res = sb.tile([P, n], F32, name="res%d" % a)
            nc.scalar.copy(res[:], acc[:])
            nc.sync.dma_start(out[:, a:b], res[:])
